import numpy as np
import ml_dtypes


def mxq(x, axis, fmt="e4m3"):
    dtype, down = {"e4m3": (ml_dtypes.float8_e4m3fn, 7), "e5m2": (ml_dtypes.float8_e5m2, 14)}[fmt]
    v = np.moveaxis(np.asarray(x, np.float32).astype(ml_dtypes.bfloat16).astype(np.float64), axis, -1)
    blocks = v.reshape(v.shape[:-1] + (-1, 32))
    amax = np.abs(blocks).max(-1, keepdims=True)
    byte = np.maximum(np.where(amax > 0, np.frexp(amax)[1] - 1 + 127, 0) - down, 1)
    scale = np.exp2(byte - 127.0)
    codes = (blocks / scale).astype(np.float32).astype(dtype).astype(np.float64)
    return np.moveaxis((codes * scale).reshape(v.shape), -1, axis)


WIDE = False


def mx_kscale(k):
    if not WIDE:
        return np.ones(k)
    levels = np.array([10, -10, 5, -5, 0])
    if k % 512:
        return np.exp2(np.random.permutation(np.resize(levels, k // 32))).repeat(32)
    a = np.empty((k // 512, 16))
    for p in range(k // 512):
        a[p, :8] = np.random.permutation(np.resize(levels, 8))
        for g in range(8):
            far = levels[np.abs(levels - a[p, g]) >= 10]
            a[p, g + 8] = far[np.random.randint(len(far))]
    return np.exp2(a.ravel()).repeat(32)


BF16 = ml_dtypes.bfloat16


def bf(x):
    return np.asarray(x, np.float32).astype(BF16)


def f64(x):
    return np.asarray(x).astype(np.float64)


M, N, R = 512, 8192, 512


def _pos(t):
    return np.maximum(t, 0.0)


def _neg(t):
    return np.maximum(-t, 0.0)


def draw0():
    u = mx_kscale(M)
    t = mx_kscale(R)
    return {
        "x": bf(np.random.standard_normal((M, N)) * u[:, None]),
        "f": bf(np.random.standard_normal((M, R)) / np.sqrt(M) * u[:, None]),
        "w": bf(np.random.uniform(0.5, 1.5, M) / (u * u)),
        "g": bf(np.random.uniform(0.2, 1.8, (N, R))),
        "p": bf(np.random.standard_normal(R) * t),
        "q": bf((1.0 + 0.2 * np.random.standard_normal(R)) / t),
    }


def core(x, f, w, g, p, q):
    x, f, w, g, p, q = f64(x), f64(f), f64(w), f64(g), f64(p), f64(q)
    fw = mxq(w[:, None] * f, 0, "e4m3")
    a = mxq(x, 0, "e4m3").T @ fw
    b = q[:, None] * (mxq(f, 0, "e4m3").T @ fw)
    c = mxq(g * p[None, :], 1, "e4m3") @ mxq(b, 0, "e4m3")
    s = np.where(p >= 0, 1.0, -1.0)
    sa = a * s[None, :]
    sc = c * s[None, :]
    num = _pos(sa) + _neg(sc) + 0.5
    den = _neg(sa) + _pos(sc) + 0.5
    return g * np.sqrt(num / den)


def e4m3fn_bytes(y):
    return np.clip(np.asarray(y, np.float64), -448.0, 448.0).astype(np.float32).astype(ml_dtypes.float8_e4m3fn).view(np.uint8)


def e4m3fn_values(b):
    return np.asarray(b, np.uint8).view(ml_dtypes.float8_e4m3fn).astype(np.float64)


def setup_inputs():
    d = draw0()
    x0 = np.asarray(d['x']).astype(np.float64)
    s = (np.max(np.abs(x0), axis=(1,), keepdims=True) / 448.0).astype(np.float32)
    out = {}
    for k, v in d.items():
        if k == 'x':
            out['x_bytes'] = e4m3fn_bytes(x0 / s.astype(np.float64))
            out['x_scale'] = s
        else:
            out[k] = v
    return out


def reference(x_bytes, x_scale, f, w, g, p, q):
    return core(e4m3fn_values(x_bytes) * x_scale.astype(np.float64), f, w, g, p, q)

@@ -1,0 +1,284 @@
+from contextlib import ExitStack
+
+import concourse.mybir as mybir
+from concourse.masks import make_identity
+
+M, N, R = 512, 8192, 512
+FLOPS = 2 * M * N * R + 2 * M * R * R + 2 * N * R * R
+
+F32 = mybir.dt.float32
+BF16 = mybir.dt.bfloat16
+U32 = mybir.dt.uint32
+U8 = mybir.dt.uint8
+FP8 = mybir.dt.float8_e4m3fn
+FP8X4 = mybir.dt.float8_e4m3fn_x4
+ALU = mybir.AluOpType
+ACT = mybir.ActivationFunctionType
+
+P = 128
+T = 4
+PAIRS = N // 256
+BATCHES = [4, 8, 8, 8, 4]
+DIRECT = 6
+LEAD = 6
+
+
+def tile_weightedsignedseminmfupdate_t_kernel(tc, x_bytes, x_scale, f, w, g, p, q, out):
+    nc = tc.nc
+    with ExitStack() as ctx:
+        keep = ctx.enter_context(tc.tile_pool(name="keep", bufs=1))
+        work = ctx.enter_context(tc.tile_pool(name="work", bufs=3))
+        psum = ctx.enter_context(tc.psum_pool(name="psum", bufs=2))
+        ctx.enter_context(tc.manual_schedule())
+
+        x_tiles = {}
+        g_tiles = {}
+        wide = {}
+        gp_tiles = {}
+        gi_tiles = {}
+        xi_tiles = {}
+        mx = {}
+        num = {}
+        den = {}
+
+        def load_x(h, parts):
+            xt = keep.tile([P, T, 1024], U8, tag="x", name="xbytes", bufs=8)
+            x_tiles[h] = xt
+            wdt = 1024 // parts
+            for i in range(parts):
+                src_ap = x_bytes[:, h * 1024 + i * wdt : h * 1024 + (i + 1) * wdt].rearrange("(p t) n -> p t n", t=T)
+                nc.sync.dma_start(out=xt[:, :, i * wdt : (i + 1) * wdt], in_=src_ap)
+
+        def load_g(k):
+            gt = work.tile([P, 2, R], BF16, tag="g", name="gin", bufs=LEAD + 4)
+            g_tiles[k] = gt
+            nc.sync.dma_start(out=gt[:], in_=g[256 * k : 256 * k + 256, :].rearrange("(j p) r -> p j r", p=P))
+
+        f_in = keep.tile([P, T, R], BF16, tag="four_k", name="f_in", bufs=4)
+        nc.sync.dma_start(out=f_in[:], in_=f.rearrange("(p t) r -> p t r", t=T))
+        w_col = keep.tile([P, T], BF16, tag="w_col", name="w_col")
+        nc.sync.dma_start(out=w_col[:], in_=w.rearrange("(p t) -> p t", t=T))
+        p_row = keep.tile([P, 2, R], BF16, tag="p_row", name="p_row")
+        nc.sync.dma_start(out=p_row[:, 0, :], in_=p.partition_broadcast(P))
+        xs = keep.tile([P, T], F32, tag="xs", name="xs")
+        nc.sync.dma_start(out=xs[:], in_=x_scale.rearrange("(p t) o -> p (t o)", t=T))
+        load_x(0, 2)
+        load_g(0)
+        q_col = keep.tile([P, T], BF16, tag="q_col", name="q_col")
+        nc.sync.dma_start(out=q_col[:], in_=q.rearrange("(p t) -> p t", t=T))
+        load_g(1)
+        load_g(2)
+        load_x(1, 1)
+        load_g(3)
+        load_g(4)
+        load_g(5)
+        for h in range(2, 8):
+            load_x(h, 1)
+
+        half = keep.tile([P, 1], F32, tag="half", name="half")
+        nc.gpsimd.memset(half[:], 0.5)
+        ident_f = keep.tile([P, P], F32, tag="ident_f", name="ident_f")
+        make_identity(nc, ident_f[:])
+        ident_b = keep.tile([P, P], BF16, tag="ident_b", name="ident_b")
+        make_identity(nc, ident_b[:])
+        warm = keep.tile([P, 1], F32, tag="warm", name="warm")
+        nc.scalar.activation(out=warm[:], in_=half[:], func=ACT.Sqrt)
+
+        def widen(c, ts, on_scalar):
+            if c not in wide:
+                wide[c] = work.tile([P, T, 512], BF16, tag="wide", name="wide", bufs=2)
+            xt = x_tiles[c // 2]
+            c0 = 512 * (c % 2)
+            for t in ts:
+                src_ap = xt[:, t, c0 : c0 + 512].bitcast(FP8)
+                if on_scalar:
+                    nc.scalar.activation(out=wide[c][:, t, :], in_=src_ap, func=ACT.Copy, scale=xs[:, t : t + 1])
+                else:
+                    nc.vector.tensor_scalar(out=wide[c][:, t, :], in0=src_ap, scalar1=xs[:, t : t + 1], scalar2=None, op0=ALU.mult)
+
+        def gmul(k):
+            gp_tiles[k] = work.tile([P, 2, R], BF16, tag="gp", name="gp", bufs=3)
+            nc.vector.tensor_tensor(out=gp_tiles[k][:], in0=g_tiles[k][:], in1=p_row[:], op=ALU.mult)
+
+        def turn(k):
+            bank = psum.tile([P, 2, 2, P], F32, tag="gt", name="gt", bufs=1)
+            words = gp_tiles[k][:].rearrange("p j r -> p (j r)").bitcast(F32)
+            for j in range(2):
+                for u in range(2):
+                    nc.tensor.transpose(bank[:, j, u, :], words[:, 256 * j + u : 256 * (j + 1) : 2], ident_f[:])
+            gi_tiles[k] = work.tile([P, 1024], BF16, tag="gi", name="gi", bufs=3, align_bytes=64)
+            nc.scalar.copy(
+                out=gi_tiles[k][:].bitcast(F32).rearrange("p (j n u) -> p j n u", j=2, u=2),
+                in_=bank[:].rearrange("p j u n -> p j n u"),
+            )
+
+        def weave(k):
+            wd = wide[k // 2]
+            c0 = 256 * (k % 2)
+            xi_tiles[k] = work.tile([P, 1024], BF16, tag="xi", name="xi", bufs=3, align_bytes=64)
+            if k < DIRECT:
+                nc.scalar.copy(
+                    out=xi_tiles[k][:].rearrange("p (n t) -> p n t", t=T),
+                    in_=wd[:, :, c0 : c0 + 256].rearrange("p t n -> p n t"),
+                )
+            else:
+                bank = psum.tile([P, 1024], BF16, tag="xw", name="xw", bufs=1)
+                for j in range(2):
+                    nc.tensor.matmul(
+                        bank[:, 512 * j : 512 * j + 512],
+                        lhsT=ident_b[:],
+                        rhs=wd[:, :, c0 + 128 * j : c0 + 128 * j + 128].rearrange("p t n -> p n t"),
+                        start=True,
+                        stop=True,
+                    )
+                nc.scalar.copy(out=xi_tiles[k][:], in_=bank[:])
+
+        def quantise(name, src_tile, width, pool, bufs):
+            codes = pool.tile([P, width // 4], U32, tag=name + "_codes", name="codes", bufs=bufs, align_bytes=64)
+            scales = pool.tile([P, width // 4], U8, tag=name + "_scales", name="scales", bufs=bufs, align_bytes=64)
+            nc.vector.quantize_mx(out=codes[:].bitcast(FP8X4), scales=scales[:], in_=src_tile[:])
+            return codes, scales
+
+        def quant(k):
+            mx[k] = (quantise("gq", gi_tiles[k], 1024, work, 3), quantise("xq", xi_tiles[k], 1024, work, 3))
+
+        def mm(bank, left, cols, right, start, stop):
+            nc.tensor.matmul_mx(
+                out=bank[:],
+                lhsT=left[0][:, cols].bitcast(FP8X4),
+                lhsT_scale=left[1][:, cols],
+                rhs=right[0][:].bitcast(FP8X4),
+                rhs_scale=right[1][:],
+                start=start,
+                stop=stop,
+            )
+
+        def products(k):
+            gq, xq = mx[k]
+            res = []
+            for j in range(2):
+                cols = slice(128 * j, 128 * j + 128)
+                bu = psum.tile([P, R], F32, tag="u", name="bu", bufs=2)
+                bd = psum.tile([P, R], F32, tag="d", name="bd", bufs=2)
+                bv = psum.tile([P, R], F32, tag="v", name="bv", bufs=2)
+                mm(bu, xq, cols, fw_q, True, True)
+                mm(bd, xq, cols, fw_q, True, False)
+                mm(bv, gq, cols, b_q, True, True)
+                mm(bd, gq, cols, b_q, False, True)
+                a = work.tile([P, R], F32, tag="a", name="a", bufs=4)
+                nc.scalar.activation(out=a[:], in_=bu[:], func=ACT.Relu)
+                res.append((a, bv, bd))
+            return res
+
+        def parts(k, res):
+            num[k] = work.tile([P, 2, R], F32, tag="num", name="num", bufs=12)
+            den[k] = work.tile([P, 2, R], F32, tag="den", name="den", bufs=12)
+            for j in range(2):
+                a, bv, bd = res[j]
+                nc.vector.scalar_tensor_tensor(out=num[k][:, j, :], in0=bv[:], scalar=0.0, in1=a[:], op0=ALU.max, op1=ALU.add)
+            for j in range(2):
+                a, bv, bd = res[j]
+                nc.vector.tensor_tensor(out=den[k][:, j, :], in0=num[k][:, j, :], in1=bd[:], op=ALU.subtract)
+
+        batch_of = {}
+        k0 = 0
+        for b, size in enumerate(BATCHES):
+            for i in range(size):
+                batch_of[k0 + i] = b
+            k0 += size
+
+        def root(tile_ap, is_num):
+            nc.scalar.activation(out=tile_ap, in_=tile_ap, func=ACT.Sqrt if is_num else ACT.Abs_reciprocal_sqrt, bias=half[:])
+
+        def first(k):
+            is_num = batch_of[k] % 2 == 0
+            e = num[k] if is_num else den[k]
+            root(e[:], is_num)
+            for j in range(2):
+                nc.gpsimd.tensor_tensor(out=e[:, j, :], in0=e[:, j, :], in1=g_tiles[k][:, j, :], op=ALU.mult)
+
+        def second(k):
+            is_num = batch_of[k] % 2 == 0
+            root((den[k] if is_num else num[k])[:], not is_num)
+
+        def finish(k):
+            is_num = batch_of[k] % 2 == 0
+            e, h = (num[k], den[k]) if is_num else (den[k], num[k])
+            nc.vector.tensor_tensor(out=e[:], in0=e[:], in1=h[:], op=ALU.mult)
+            nc.sync.dma_start(out=out[256 * k : 256 * k + 256, :].rearrange("(j p) r -> p j r", p=P), in_=e[:])
+
+        sgn = keep.tile([P, R], BF16, tag="sgn", name="sgn")
+        nc.vector.tensor_scalar(out=sgn[:], in0=p_row[:, 0, :], scalar1=0.0, scalar2=2.0, op0=ALU.is_ge, op1=ALU.mult)
+        nc.vector.tensor_copy(out=p_row[:, 1, :], in_=p_row[:, 0, :])
+        nc.vector.tensor_scalar(out=sgn[:], in0=sgn[:], scalar1=-1.0, scalar2=None, op0=ALU.add)
+        qn = keep.tile([P, T], F32, tag="qn", name="qn")
+        nc.vector.tensor_scalar(out=qn[:], in0=q_col[:], scalar1=-1.0, scalar2=None, op0=ALU.mult)
+
+        fi = keep.tile([P, T * R], BF16, tag="four_k2", name="fi", bufs=3, align_bytes=64)
+        nc.scalar.copy(
+            out=fi[:].rearrange("p (t m j) -> p t m j", t=T, j=T),
+            in_=f_in[:].rearrange("p j (m t) -> p t m j", t=T),
+        )
+        fwt = keep.tile([P, T, R], BF16, tag="four_k", name="fwt", bufs=4)
+        for t in range(T):
+            nc.vector.scalar_tensor_tensor(out=fwt[:, t, :], in0=f_in[:, t, :], scalar=w_col[:, t : t + 1], in1=sgn[:], op0=ALU.mult, op1=ALU.mult)
+        gmul(0)
+        fwi = keep.tile([P, T * R], BF16, tag="four_k2", name="fwi", bufs=3, align_bytes=64)
+        nc.vector.tensor_copy(out=fwi[:].rearrange("p (r t) -> p r t", t=T), in_=fwt[:].rearrange("p t r -> p r t"))
+        widen(0, range(T), True)
+        weave(0)
+        turn(0)
+        gmul(1)
+        fw_q = quantise("fw", fwi, 2048, keep, 1)
+        f_q = quantise("f", fi, 2048, keep, 1)
+        gmul(2)
+        bt = keep.tile([P, T, R], BF16, tag="four_k", name="bt", bufs=4)
+        banks = []
+        for t in range(T):
+            bank = psum.tile([P, R], F32, tag="u" if t % 2 == 0 else "v", name="bb", bufs=2)
+            mm(bank, f_q, slice(128 * t, 128 * t + 128), fw_q, True, True)
+            if t % 2 == 0:
+                nc.scalar.activation(out=bt[:, t, :], in_=bank[:], func=ACT.Copy, scale=qn[:, t : t + 1])
+            else:
+                nc.vector.tensor_scalar(out=bt[:, t, :], in0=bank[:], scalar1=qn[:, t : t + 1], scalar2=None, op0=ALU.mult)
+        bi = keep.tile([P, T * R], BF16, tag="four_k2", name="bi", bufs=3, align_bytes=64)
+        nc.vector.tensor_copy(out=bi[:].rearrange("p (r t) -> p r t", t=T), in_=bt[:].rearrange("p t r -> p r t"))
+        turn(1)
+        weave(1)
+        quant(0)
+        b_q = quantise("b", bi, 2048, keep, 1)
+        widen(1, range(T), True)
+
+        starts = [sum(BATCHES[:b]) for b in range(len(BATCHES) + 1)]
+        todo = {}
+        for b in range(len(BATCHES)):
+            size = BATCHES[b]
+            room = BATCHES[b + 1] if b + 1 < len(BATCHES) else size
+            for i in range(size):
+                step = starts[b + 1] + 1 + (i * room) // size
+                todo.setdefault(step, []).append(starts[b] + i)
+        last = max(todo)
+        pending = []
+        for s in range(last + 2):
+            if s + LEAD < PAIRS:
+                load_g(s + LEAD)
+            res = products(s) if s < PAIRS else None
+            if s + 1 < PAIRS:
+                quant(s + 1)
+            if s + 2 < PAIRS:
+                turn(s + 2)
+                weave(s + 2)
+            if s + 3 < PAIRS:
+                gmul(s + 3)
+            c = (s + 4) // 2
+            if c < N // 512:
+                widen(c, (0, 1) if s % 2 == 0 else (2, 3), False)
+            if res is not None:
+                parts(s, res)
+            if 1 <= s <= PAIRS:
+                first(s - 1)
+            for k in pending:
+                finish(k)
+            pending = todo.get(s, [])
+            for k in pending:
+                second(k)

@@ -18,7 +18,7 @@ ACT = mybir.ActivationFunctionType
 P = 128
 T = 4
 PAIRS = N // 256
-BATCHES = [4, 8, 8, 8, 4]
+BATCHES = [4, 8, 8, 6, 4, 2]
 DIRECT = 6
 LEAD = 6
 
@@ -81,6 +81,7 @@ def tile_weightedsignedseminmfupdate_t_kernel(tc, x_bytes, x_scale, f, w, g, p, 
         make_identity(nc, ident_f[:])
         ident_b = keep.tile([P, P], BF16, tag="ident_b", name="ident_b")
         make_identity(nc, ident_b[:])
+        touch = keep.tile([P, 1], F32, tag="touch", name="touch")
         warm = keep.tile([P, 1], F32, tag="warm", name="warm")
         nc.scalar.activation(out=warm[:], in_=half[:], func=ACT.Sqrt)
 
@@ -156,18 +157,21 @@ def tile_weightedsignedseminmfupdate_t_kernel(tc, x_bytes, x_scale, f, w, g, p, 
         def products(k):
             gq, xq = mx[k]
             res = []
+            all_cols = [slice(0, 128), slice(128, 256)]
+            relus = []
             for j in range(2):
-                cols = slice(128 * j, 128 * j + 128)
                 bu = psum.tile([P, R], F32, tag="u", name="bu", bufs=2)
-                bd = psum.tile([P, R], F32, tag="d", name="bd", bufs=2)
-                bv = psum.tile([P, R], F32, tag="v", name="bv", bufs=2)
-                mm(bu, xq, cols, fw_q, True, True)
-                mm(bd, xq, cols, fw_q, True, False)
-                mm(bv, gq, cols, b_q, True, True)
-                mm(bd, gq, cols, b_q, False, True)
+                mm(bu, xq, all_cols[j], fw_q, True, True)
                 a = work.tile([P, R], F32, tag="a", name="a", bufs=4)
                 nc.scalar.activation(out=a[:], in_=bu[:], func=ACT.Relu)
-                res.append((a, bv, bd))
+                relus.append(a)
+            for j in range(2):
+                bd = psum.tile([P, R], F32, tag="d", name="bd", bufs=2)
+                bv = psum.tile([P, R], F32, tag="v", name="bv", bufs=2)
+                mm(bd, xq, all_cols[j], fw_q, True, False)
+                mm(bv, gq, all_cols[j], b_q, True, True)
+                mm(bd, gq, all_cols[j], b_q, False, True)
+                res.append((relus[j], bv, bd))
             return res
 
         def parts(k, res):
@@ -194,6 +198,11 @@ def tile_weightedsignedseminmfupdate_t_kernel(tc, x_bytes, x_scale, f, w, g, p, 
             is_num = batch_of[k] % 2 == 0
             e = num[k] if is_num else den[k]
             root(e[:], is_num)
+
+        def times_g(k):
+            is_num = batch_of[k] % 2 == 0
+            e = num[k] if is_num else den[k]
+            nc.vector.tensor_copy(out=touch[:], in_=e[:, 0, 0:1])
             for j in range(2):
                 nc.gpsimd.tensor_tensor(out=e[:, j, :], in0=e[:, j, :], in1=g_tiles[k][:, j, :], op=ALU.mult)
 
@@ -263,6 +272,11 @@ def tile_weightedsignedseminmfupdate_t_kernel(tc, x_bytes, x_scale, f, w, g, p, 
             if s + LEAD < PAIRS:
                 load_g(s + LEAD)
             res = products(s) if s < PAIRS else None
+            if 1 <= s <= PAIRS:
+                first(s - 1)
+            new = todo.get(s, [])
+            for k in new:
+                second(k)
             if s + 1 < PAIRS:
                 quant(s + 1)
             if s + 2 < PAIRS:
@@ -272,13 +286,15 @@ def tile_weightedsignedseminmfupdate_t_kernel(tc, x_bytes, x_scale, f, w, g, p, 
                 gmul(s + 3)
             c = (s + 4) // 2
             if c < N // 512:
-                widen(c, (0, 1) if s % 2 == 0 else (2, 3), False)
-            if res is not None:
-                parts(s, res)
-            if 1 <= s <= PAIRS:
-                first(s - 1)
+                if s % 2 == 0:
+                    widen(c, (0, 1), False)
+                else:
+                    widen(c, (2,), False)
+                    widen(c, (3,), True)
             for k in pending:
                 finish(k)
-            pending = todo.get(s, [])
-            for k in pending:
-                second(k)
+            pending = new
+            if 1 <= s <= PAIRS:
+                times_g(s - 1)
+            if res is not None:
+                parts(s, res)

@@ -42,7 +42,7 @@ def tile_weightedsignedseminmfupdate_t_kernel(tc, x_bytes, x_scale, f, w, g, p, 
         den = {}
 
         def load_x(h, parts):
-            xt = keep.tile([P, T, 1024], U8, tag="x", name="xbytes", bufs=8)
+            xt = keep.tile([P, T, 1024], U8, tag="x", name="xbytes", bufs=5)
             x_tiles[h] = xt
             wdt = 1024 // parts
             for i in range(parts):
@@ -50,7 +50,7 @@ def tile_weightedsignedseminmfupdate_t_kernel(tc, x_bytes, x_scale, f, w, g, p, 
                 nc.sync.dma_start(out=xt[:, :, i * wdt : (i + 1) * wdt], in_=src_ap)
 
         def load_g(k):
-            gt = work.tile([P, 2, R], BF16, tag="g", name="gin", bufs=LEAD + 4)
+            gt = work.tile([P, 2, R], BF16, tag="g", name="gin", bufs=LEAD + 5)
             g_tiles[k] = gt
             nc.sync.dma_start(out=gt[:], in_=g[256 * k : 256 * k + 256, :].rearrange("(j p) r -> p j r", p=P))
 
@@ -72,7 +72,7 @@ def tile_weightedsignedseminmfupdate_t_kernel(tc, x_bytes, x_scale, f, w, g, p, 
         load_g(3)
         load_g(4)
         load_g(5)
-        for h in range(2, 8):
+        for h in range(2, 5):
             load_x(h, 1)
 
         half = keep.tile([P, 1], F32, tag="half", name="half")
@@ -107,7 +107,7 @@ def tile_weightedsignedseminmfupdate_t_kernel(tc, x_bytes, x_scale, f, w, g, p, 
             for j in range(2):
                 for u in range(2):
                     nc.tensor.transpose(bank[:, j, u, :], words[:, 256 * j + u : 256 * (j + 1) : 2], ident_f[:])
-            gi_tiles[k] = work.tile([P, 1024], BF16, tag="gi", name="gi", bufs=3, align_bytes=64)
+            gi_tiles[k] = work.tile([P, 1024], BF16, tag="gi", name="gi", bufs=4, align_bytes=64)
             nc.scalar.copy(
                 out=gi_tiles[k][:].bitcast(F32).rearrange("p (j n u) -> p j n u", j=2, u=2),
                 in_=bank[:].rearrange("p j u n -> p j n u"),
@@ -116,7 +116,7 @@ def tile_weightedsignedseminmfupdate_t_kernel(tc, x_bytes, x_scale, f, w, g, p, 
         def weave(k):
             wd = wide[k // 2]
             c0 = 256 * (k % 2)
-            xi_tiles[k] = work.tile([P, 1024], BF16, tag="xi", name="xi", bufs=3, align_bytes=64)
+            xi_tiles[k] = work.tile([P, 1024], BF16, tag="xi", name="xi", bufs=4, align_bytes=64)
             if k < DIRECT:
                 nc.scalar.copy(
                     out=xi_tiles[k][:].rearrange("p (n t) -> p n t", t=T),
@@ -165,18 +165,22 @@ def tile_weightedsignedseminmfupdate_t_kernel(tc, x_bytes, x_scale, f, w, g, p, 
                 a = work.tile([P, R], F32, tag="a", name="a", bufs=4)
                 nc.scalar.activation(out=a[:], in_=bu[:], func=ACT.Relu)
                 relus.append(a)
+            bvs = []
+            for j in range(2):
+                bv = psum.tile([P, R], F32, tag="v", name="bv", bufs=2)
+                mm(bv, gq, all_cols[j], b_q, True, True)
+                bvs.append(bv)
             for j in range(2):
                 bd = psum.tile([P, R], F32, tag="d", name="bd", bufs=2)
-                bv = psum.tile([P, R], F32, tag="v", name="bv", bufs=2)
+                bv = bvs[j]
                 mm(bd, xq, all_cols[j], fw_q, True, False)
-                mm(bv, gq, all_cols[j], b_q, True, True)
                 mm(bd, gq, all_cols[j], b_q, False, True)
                 res.append((relus[j], bv, bd))
             return res
 
         def parts(k, res):
-            num[k] = work.tile([P, 2, R], F32, tag="num", name="num", bufs=12)
-            den[k] = work.tile([P, 2, R], F32, tag="den", name="den", bufs=12)
+            num[k] = work.tile([P, 2, R], F32, tag="num", name="num", bufs=13)
+            den[k] = work.tile([P, 2, R], F32, tag="den", name="den", bufs=13)
             for j in range(2):
                 a, bv, bd = res[j]
                 nc.vector.scalar_tensor_tensor(out=num[k][:, j, :], in0=bv[:], scalar=0.0, in1=a[:], op0=ALU.max, op1=ALU.add)
@@ -255,8 +259,12 @@ def tile_weightedsignedseminmfupdate_t_kernel(tc, x_bytes, x_scale, f, w, g, p, 
         turn(1)
         weave(1)
         quant(0)
+        gmul(3)
         b_q = quantise("b", bi, 2048, keep, 1)
-        widen(1, range(T), True)
+        widen(1, range(T), False)
+        turn(2)
+        weave(2)
+        widen(2, (0, 1), False)
 
         starts = [sum(BATCHES[:b]) for b in range(len(BATCHES) + 1)]
         todo = {}
@@ -271,22 +279,24 @@ def tile_weightedsignedseminmfupdate_t_kernel(tc, x_bytes, x_scale, f, w, g, p, 
         for s in range(last + 2):
             if s + LEAD < PAIRS:
                 load_g(s + LEAD)
+            if s % 4 == 0 and 5 <= s // 4 + 5 < 8:
+                load_x(s // 4 + 5, 1)
             res = products(s) if s < PAIRS else None
-            if 1 <= s <= PAIRS:
-                first(s - 1)
             new = todo.get(s, [])
             for k in new:
                 second(k)
+            if 1 <= s <= PAIRS:
+                first(s - 1)
             if s + 1 < PAIRS:
                 quant(s + 1)
-            if s + 2 < PAIRS:
-                turn(s + 2)
-                weave(s + 2)
             if s + 3 < PAIRS:
-                gmul(s + 3)
-            c = (s + 4) // 2
+                turn(s + 3)
+                weave(s + 3)
+            if s + 4 < PAIRS:
+                gmul(s + 4)
+            c = (s + 5) // 2
             if c < N // 512:
-                if s % 2 == 0:
+                if s % 2 == 1:
                     widen(c, (0, 1), False)
                 else:
                     widen(c, (2,), False)
@@ -294,7 +304,7 @@ def tile_weightedsignedseminmfupdate_t_kernel(tc, x_bytes, x_scale, f, w, g, p, 
             for k in pending:
                 finish(k)
             pending = new
-            if 1 <= s <= PAIRS:
-                times_g(s - 1)
+            if 2 <= s <= PAIRS + 1:
+                times_g(s - 2)
             if res is not None:
                 parts(s, res)

@@ -18,9 +18,16 @@ ACT = mybir.ActivationFunctionType
 P = 128
 T = 4
 PAIRS = N // 256
-BATCHES = [4, 8, 8, 6, 4, 2]
+BATCHES = [5, 9, 9, 7, 2]
 DIRECT = 6
-LEAD = 6
+LEAD = 7
+HOLD = 18
+V_TURN = tuple(range(24, 32))
+SW1 = True
+SW2 = False
+G_OUT = (0, 1, 2)
+TAIL = 24
+T1_TAIL = 30
 
 
 def tile_weightedsignedseminmfupdate_t_kernel(tc, x_bytes, x_scale, f, w, g, p, q, out):
@@ -37,12 +44,13 @@ def tile_weightedsignedseminmfupdate_t_kernel(tc, x_bytes, x_scale, f, w, g, p, 
         gp_tiles = {}
         gi_tiles = {}
         xi_tiles = {}
+        turned = {}
         mx = {}
         num = {}
         den = {}
 
         def load_x(h, parts):
-            xt = keep.tile([P, T, 1024], U8, tag="x", name="xbytes", bufs=5)
+            xt = keep.tile([P, T, 1024], U8, tag="x", name="xbytes", bufs=3)
             x_tiles[h] = xt
             wdt = 1024 // parts
             for i in range(parts):
@@ -50,16 +58,16 @@ def tile_weightedsignedseminmfupdate_t_kernel(tc, x_bytes, x_scale, f, w, g, p, 
                 nc.sync.dma_start(out=xt[:, :, i * wdt : (i + 1) * wdt], in_=src_ap)
 
         def load_g(k):
-            gt = work.tile([P, 2, R], BF16, tag="g", name="gin", bufs=LEAD + 5)
+            gt = work.tile([P, 2, R], BF16, tag="g", name="gin", bufs=LEAD + 3)
             g_tiles[k] = gt
             nc.sync.dma_start(out=gt[:], in_=g[256 * k : 256 * k + 256, :].rearrange("(j p) r -> p j r", p=P))
 
-        f_in = keep.tile([P, T, R], BF16, tag="four_k", name="f_in", bufs=4)
-        nc.sync.dma_start(out=f_in[:], in_=f.rearrange("(p t) r -> p t r", t=T))
+        f_in = work.tile([P, T, R], BF16, tag="num", name="f_in", bufs=HOLD, align_bytes=64)
         w_col = keep.tile([P, T], BF16, tag="w_col", name="w_col")
         nc.sync.dma_start(out=w_col[:], in_=w.rearrange("(p t) -> p t", t=T))
         p_row = keep.tile([P, 2, R], BF16, tag="p_row", name="p_row")
         nc.sync.dma_start(out=p_row[:, 0, :], in_=p.partition_broadcast(P))
+        nc.sync.dma_start(out=f_in[:], in_=f.rearrange("(p t) r -> p t r", t=T))
         xs = keep.tile([P, T], F32, tag="xs", name="xs")
         nc.sync.dma_start(out=xs[:], in_=x_scale.rearrange("(p t) o -> p (t o)", t=T))
         load_x(0, 2)
@@ -70,10 +78,9 @@ def tile_weightedsignedseminmfupdate_t_kernel(tc, x_bytes, x_scale, f, w, g, p, 
         load_g(2)
         load_x(1, 1)
         load_g(3)
-        load_g(4)
-        load_g(5)
-        for h in range(2, 5):
-            load_x(h, 1)
+        load_x(2, 1)
+        for k in range(4, LEAD):
+            load_g(k)
 
         half = keep.tile([P, 1], F32, tag="half", name="half")
         nc.gpsimd.memset(half[:], 0.5)
@@ -81,7 +88,6 @@ def tile_weightedsignedseminmfupdate_t_kernel(tc, x_bytes, x_scale, f, w, g, p, 
         make_identity(nc, ident_f[:])
         ident_b = keep.tile([P, P], BF16, tag="ident_b", name="ident_b")
         make_identity(nc, ident_b[:])
-        touch = keep.tile([P, 1], F32, tag="touch", name="touch")
         warm = keep.tile([P, 1], F32, tag="warm", name="warm")
         nc.scalar.activation(out=warm[:], in_=half[:], func=ACT.Sqrt)
 
@@ -97,9 +103,9 @@ def tile_weightedsignedseminmfupdate_t_kernel(tc, x_bytes, x_scale, f, w, g, p, 
                 else:
                     nc.vector.tensor_scalar(out=wide[c][:, t, :], in0=src_ap, scalar1=xs[:, t : t + 1], scalar2=None, op0=ALU.mult)
 
-        def gmul(k):
+        def gmul(k, engine):
             gp_tiles[k] = work.tile([P, 2, R], BF16, tag="gp", name="gp", bufs=3)
-            nc.vector.tensor_tensor(out=gp_tiles[k][:], in0=g_tiles[k][:], in1=p_row[:], op=ALU.mult)
+            engine.tensor_tensor(out=gp_tiles[k][:], in0=g_tiles[k][:], in1=p_row[:], op=ALU.mult)
 
         def turn(k):
             bank = psum.tile([P, 2, 2, P], F32, tag="gt", name="gt", bufs=1)
@@ -108,7 +114,11 @@ def tile_weightedsignedseminmfupdate_t_kernel(tc, x_bytes, x_scale, f, w, g, p, 
                 for u in range(2):
                     nc.tensor.transpose(bank[:, j, u, :], words[:, 256 * j + u : 256 * (j + 1) : 2], ident_f[:])
             gi_tiles[k] = work.tile([P, 1024], BF16, tag="gi", name="gi", bufs=4, align_bytes=64)
-            nc.scalar.copy(
+            turned[k] = bank
+
+        def emit_turned(k, copy):
+            bank = turned[k]
+            copy(
                 out=gi_tiles[k][:].bitcast(F32).rearrange("p (j n u) -> p j n u", j=2, u=2),
                 in_=bank[:].rearrange("p j u n -> p j n u"),
             )
@@ -159,17 +169,16 @@ def tile_weightedsignedseminmfupdate_t_kernel(tc, x_bytes, x_scale, f, w, g, p, 
             res = []
             all_cols = [slice(0, 128), slice(128, 256)]
             relus = []
-            for j in range(2):
-                bu = psum.tile([P, R], F32, tag="u", name="bu", bufs=2)
-                mm(bu, xq, all_cols[j], fw_q, True, True)
-                a = work.tile([P, R], F32, tag="a", name="a", bufs=4)
-                nc.scalar.activation(out=a[:], in_=bu[:], func=ACT.Relu)
-                relus.append(a)
             bvs = []
             for j in range(2):
                 bv = psum.tile([P, R], F32, tag="v", name="bv", bufs=2)
                 mm(bv, gq, all_cols[j], b_q, True, True)
                 bvs.append(bv)
+                bu = psum.tile([P, R], F32, tag="u", name="bu", bufs=2)
+                mm(bu, xq, all_cols[j], fw_q, True, True)
+                a = work.tile([P, R], F32, tag="a", name="a", bufs=4)
+                nc.scalar.activation(out=a[:], in_=bu[:], func=ACT.Relu)
+                relus.append(a)
             for j in range(2):
                 bd = psum.tile([P, R], F32, tag="d", name="bd", bufs=2)
                 bv = bvs[j]
@@ -179,8 +188,8 @@ def tile_weightedsignedseminmfupdate_t_kernel(tc, x_bytes, x_scale, f, w, g, p, 
             return res
 
         def parts(k, res):
-            num[k] = work.tile([P, 2, R], F32, tag="num", name="num", bufs=13)
-            den[k] = work.tile([P, 2, R], F32, tag="den", name="den", bufs=13)
+            num[k] = work.tile([P, 2, R], F32, tag="num", name="num", bufs=HOLD, align_bytes=64)
+            den[k] = work.tile([P, 2, R], F32, tag="den", name="den", bufs=HOLD, align_bytes=64)
             for j in range(2):
                 a, bv, bd = res[j]
                 nc.vector.scalar_tensor_tensor(out=num[k][:, j, :], in0=bv[:], scalar=0.0, in1=a[:], op0=ALU.max, op1=ALU.add)
@@ -206,9 +215,9 @@ def tile_weightedsignedseminmfupdate_t_kernel(tc, x_bytes, x_scale, f, w, g, p, 
         def times_g(k):
             is_num = batch_of[k] % 2 == 0
             e = num[k] if is_num else den[k]
-            nc.vector.tensor_copy(out=touch[:], in_=e[:, 0, 0:1])
             for j in range(2):
-                nc.gpsimd.tensor_tensor(out=e[:, j, :], in0=e[:, j, :], in1=g_tiles[k][:, j, :], op=ALU.mult)
+                engine = nc.gpsimd if k < T1_TAIL else nc.vector
+                engine.tensor_tensor(out=e[:, j, :], in0=e[:, j, :], in1=g_tiles[k][:, j, :], op=ALU.mult)
 
         def second(k):
             is_num = batch_of[k] % 2 == 0
@@ -217,8 +226,13 @@ def tile_weightedsignedseminmfupdate_t_kernel(tc, x_bytes, x_scale, f, w, g, p, 
         def finish(k):
             is_num = batch_of[k] % 2 == 0
             e, h = (num[k], den[k]) if is_num else (den[k], num[k])
-            nc.vector.tensor_tensor(out=e[:], in0=e[:], in1=h[:], op=ALU.mult)
-            nc.sync.dma_start(out=out[256 * k : 256 * k + 256, :].rearrange("(j p) r -> p j r", p=P), in_=e[:])
+            for j in range(2):
+                engine = nc.gpsimd if (2 * k + j) % 4 in G_OUT and k < TAIL else nc.vector
+                engine.tensor_tensor(out=e[:, j, :], in0=e[:, j, :], in1=h[:, j, :], op=ALU.mult)
+                if k >= PAIRS - 2:
+                    nc.sync.dma_start(out=out[256 * k + P * j : 256 * k + P * j + P, :], in_=e[:, j, :])
+            if k < PAIRS - 2:
+                nc.sync.dma_start(out=out[256 * k : 256 * k + 256, :].rearrange("(j p) r -> p j r", p=P), in_=e[:])
 
         sgn = keep.tile([P, R], BF16, tag="sgn", name="sgn")
         nc.vector.tensor_scalar(out=sgn[:], in0=p_row[:, 0, :], scalar1=0.0, scalar2=2.0, op0=ALU.is_ge, op1=ALU.mult)
@@ -227,25 +241,26 @@ def tile_weightedsignedseminmfupdate_t_kernel(tc, x_bytes, x_scale, f, w, g, p, 
         qn = keep.tile([P, T], F32, tag="qn", name="qn")
         nc.vector.tensor_scalar(out=qn[:], in0=q_col[:], scalar1=-1.0, scalar2=None, op0=ALU.mult)
 
-        fi = keep.tile([P, T * R], BF16, tag="four_k2", name="fi", bufs=3, align_bytes=64)
+        fi = work.tile([P, T * R], BF16, tag="den", name="fi", bufs=HOLD, align_bytes=64)
         nc.scalar.copy(
             out=fi[:].rearrange("p (t m j) -> p t m j", t=T, j=T),
             in_=f_in[:].rearrange("p j (m t) -> p t m j", t=T),
         )
-        fwt = keep.tile([P, T, R], BF16, tag="four_k", name="fwt", bufs=4)
+        fwt = work.tile([P, T, R], BF16, tag="num", name="fwt", bufs=HOLD, align_bytes=64)
         for t in range(T):
             nc.vector.scalar_tensor_tensor(out=fwt[:, t, :], in0=f_in[:, t, :], scalar=w_col[:, t : t + 1], in1=sgn[:], op0=ALU.mult, op1=ALU.mult)
-        gmul(0)
-        fwi = keep.tile([P, T * R], BF16, tag="four_k2", name="fwi", bufs=3, align_bytes=64)
+        gmul(0, nc.gpsimd)
+        fwi = work.tile([P, T * R], BF16, tag="den", name="fwi", bufs=HOLD, align_bytes=64)
         nc.vector.tensor_copy(out=fwi[:].rearrange("p (r t) -> p r t", t=T), in_=fwt[:].rearrange("p t r -> p r t"))
         widen(0, range(T), True)
         weave(0)
         turn(0)
-        gmul(1)
+        emit_turned(0, nc.scalar.copy)
+        gmul(1, nc.gpsimd)
         fw_q = quantise("fw", fwi, 2048, keep, 1)
         f_q = quantise("f", fi, 2048, keep, 1)
-        gmul(2)
-        bt = keep.tile([P, T, R], BF16, tag="four_k", name="bt", bufs=4)
+        gmul(2, nc.vector)
+        bt = work.tile([P, T, R], BF16, tag="num", name="bt", bufs=HOLD, align_bytes=64)
         banks = []
         for t in range(T):
             bank = psum.tile([P, R], F32, tag="u" if t % 2 == 0 else "v", name="bb", bufs=2)
@@ -254,17 +269,19 @@ def tile_weightedsignedseminmfupdate_t_kernel(tc, x_bytes, x_scale, f, w, g, p, 
                 nc.scalar.activation(out=bt[:, t, :], in_=bank[:], func=ACT.Copy, scale=qn[:, t : t + 1])
             else:
                 nc.vector.tensor_scalar(out=bt[:, t, :], in0=bank[:], scalar1=qn[:, t : t + 1], scalar2=None, op0=ALU.mult)
-        bi = keep.tile([P, T * R], BF16, tag="four_k2", name="bi", bufs=3, align_bytes=64)
+        bi = work.tile([P, T * R], BF16, tag="den", name="bi", bufs=HOLD, align_bytes=64)
         nc.vector.tensor_copy(out=bi[:].rearrange("p (r t) -> p r t", t=T), in_=bt[:].rearrange("p t r -> p r t"))
         turn(1)
+        emit_turned(1, nc.scalar.copy)
         weave(1)
         quant(0)
-        gmul(3)
+        gmul(3, nc.vector)
         b_q = quantise("b", bi, 2048, keep, 1)
-        widen(1, range(T), False)
+        widen(1, range(T), SW1)
         turn(2)
+        emit_turned(2, nc.scalar.copy)
         weave(2)
-        widen(2, (0, 1), False)
+        widen(2, (0, 1), SW2)
 
         starts = [sum(BATCHES[:b]) for b in range(len(BATCHES) + 1)]
         todo = {}
@@ -276,11 +293,12 @@ def tile_weightedsignedseminmfupdate_t_kernel(tc, x_bytes, x_scale, f, w, g, p, 
                 todo.setdefault(step, []).append(starts[b] + i)
         last = max(todo)
         pending = []
+        load_x(3, 1)
         for s in range(last + 2):
             if s + LEAD < PAIRS:
                 load_g(s + LEAD)
-            if s % 4 == 0 and 5 <= s // 4 + 5 < 8:
-                load_x(s // 4 + 5, 1)
+            if s % 4 == 3 and s // 4 + 4 < 8:
+                load_x(s // 4 + 4, 1)
             res = products(s) if s < PAIRS else None
             new = todo.get(s, [])
             for k in new:
@@ -291,16 +309,17 @@ def tile_weightedsignedseminmfupdate_t_kernel(tc, x_bytes, x_scale, f, w, g, p, 
                 quant(s + 1)
             if s + 3 < PAIRS:
                 turn(s + 3)
+                if s + 3 not in V_TURN:
+                    emit_turned(s + 3, nc.scalar.copy)
                 weave(s + 3)
             if s + 4 < PAIRS:
-                gmul(s + 4)
+                gmul(s + 4, nc.vector)
             c = (s + 5) // 2
             if c < N // 512:
                 if s % 2 == 1:
                     widen(c, (0, 1), False)
                 else:
-                    widen(c, (2,), False)
-                    widen(c, (3,), True)
+                    widen(c, (2, 3), False)
             for k in pending:
                 finish(k)
             pending = new
@@ -308,3 +327,5 @@ def tile_weightedsignedseminmfupdate_t_kernel(tc, x_bytes, x_scale, f, w, g, p, 
                 times_g(s - 2)
             if res is not None:
                 parts(s, res)
+            if s + 3 < PAIRS and s + 3 in V_TURN:
+                emit_turned(s + 3, nc.vector.tensor_copy)

@@ -22,10 +22,11 @@ BATCHES = [5, 9, 9, 7, 2]
 DIRECT = 6
 LEAD = 7
 HOLD = 18
-V_TURN = tuple(range(24, 32))
 SW1 = True
 SW2 = False
-G_OUT = (0, 1, 2)
+S_T = ((1, 2, 3), (2, 3))
+TOUCH = True
+G_OUT = (3,)
 TAIL = 24
 T1_TAIL = 30
 
@@ -41,9 +42,7 @@ def tile_weightedsignedseminmfupdate_t_kernel(tc, x_bytes, x_scale, f, w, g, p, 
         x_tiles = {}
         g_tiles = {}
         wide = {}
-        gp_tiles = {}
-        gi_tiles = {}
-        xi_tiles = {}
+        inter = {}
         turned = {}
         mx = {}
         num = {}
@@ -65,8 +64,10 @@ def tile_weightedsignedseminmfupdate_t_kernel(tc, x_bytes, x_scale, f, w, g, p, 
         f_in = work.tile([P, T, R], BF16, tag="num", name="f_in", bufs=HOLD, align_bytes=64)
         w_col = keep.tile([P, T], BF16, tag="w_col", name="w_col")
         nc.sync.dma_start(out=w_col[:], in_=w.rearrange("(p t) -> p t", t=T))
-        p_row = keep.tile([P, 2, R], BF16, tag="p_row", name="p_row")
-        nc.sync.dma_start(out=p_row[:, 0, :], in_=p.partition_broadcast(P))
+        p_row = keep.tile([P, R], BF16, tag="p_row", name="p_row")
+        nc.sync.dma_start(out=p_row[:], in_=p.partition_broadcast(P))
+        p_col = keep.tile([P, T], BF16, tag="p_col", name="p_col")
+        nc.sync.dma_start(out=p_col[:], in_=p.rearrange("(p t) -> p t", t=T))
         nc.sync.dma_start(out=f_in[:], in_=f.rearrange("(p t) r -> p t r", t=T))
         xs = keep.tile([P, T], F32, tag="xs", name="xs")
         nc.sync.dma_start(out=xs[:], in_=x_scale.rearrange("(p t) o -> p (t o)", t=T))
@@ -88,6 +89,7 @@ def tile_weightedsignedseminmfupdate_t_kernel(tc, x_bytes, x_scale, f, w, g, p, 
         make_identity(nc, ident_f[:])
         ident_b = keep.tile([P, P], BF16, tag="ident_b", name="ident_b")
         make_identity(nc, ident_b[:])
+        touch = keep.tile([P, 1], F32, tag="touch", name="touch")
         warm = keep.tile([P, 1], F32, tag="warm", name="warm")
         nc.scalar.activation(out=warm[:], in_=half[:], func=ACT.Sqrt)
 
@@ -103,33 +105,34 @@ def tile_weightedsignedseminmfupdate_t_kernel(tc, x_bytes, x_scale, f, w, g, p, 
                 else:
                     nc.vector.tensor_scalar(out=wide[c][:, t, :], in0=src_ap, scalar1=xs[:, t : t + 1], scalar2=None, op0=ALU.mult)
 
-        def gmul(k, engine):
-            gp_tiles[k] = work.tile([P, 2, R], BF16, tag="gp", name="gp", bufs=3)
-            engine.tensor_tensor(out=gp_tiles[k][:], in0=g_tiles[k][:], in1=p_row[:], op=ALU.mult)
+        def inter_tile(k):
+            if k not in inter:
+                inter[k] = work.tile([P, 2, 1024], BF16, tag="inter", name="inter", bufs=4, align_bytes=64)
+            return inter[k]
 
         def turn(k):
-            bank = psum.tile([P, 2, 2, P], F32, tag="gt", name="gt", bufs=1)
-            words = gp_tiles[k][:].rearrange("p j r -> p (j r)").bitcast(F32)
+            bank = psum.tile([P, 2, 256], F32, tag="gt", name="gt", bufs=1)
+            words = g_tiles[k][:].rearrange("p j r -> p (j r)").bitcast(F32)
             for j in range(2):
                 for u in range(2):
-                    nc.tensor.transpose(bank[:, j, u, :], words[:, 256 * j + u : 256 * (j + 1) : 2], ident_f[:])
-            gi_tiles[k] = work.tile([P, 1024], BF16, tag="gi", name="gi", bufs=4, align_bytes=64)
+                    nc.tensor.transpose(bank[:, u, 128 * j : 128 * j + 128], words[:, 256 * j + u : 256 * (j + 1) : 2], ident_f[:])
             turned[k] = bank
 
-        def emit_turned(k, copy):
-            bank = turned[k]
-            copy(
-                out=gi_tiles[k][:].bitcast(F32).rearrange("p (j n u) -> p j n u", j=2, u=2),
-                in_=bank[:].rearrange("p j u n -> p j n u"),
+        def emit_turned(k):
+            nc.vector.tensor_tensor(
+                out=inter_tile(k)[:, 0, :].rearrange("p (n u e) -> p n u e", u=2, e=2),
+                in0=turned[k][:].bitcast(BF16).rearrange("p u (n e) -> p n u e", e=2),
+                in1=p_cols[:].rearrange("p (n u e) -> p n u e", u=2, e=2),
+                op=ALU.mult,
             )
 
         def weave(k):
             wd = wide[k // 2]
             c0 = 256 * (k % 2)
-            xi_tiles[k] = work.tile([P, 1024], BF16, tag="xi", name="xi", bufs=4, align_bytes=64)
+            dst = inter_tile(k)[:, 1, :]
             if k < DIRECT:
                 nc.scalar.copy(
-                    out=xi_tiles[k][:].rearrange("p (n t) -> p n t", t=T),
+                    out=dst.rearrange("p (n t) -> p n t", t=T),
                     in_=wd[:, :, c0 : c0 + 256].rearrange("p t n -> p n t"),
                 )
             else:
@@ -142,16 +145,16 @@ def tile_weightedsignedseminmfupdate_t_kernel(tc, x_bytes, x_scale, f, w, g, p, 
                         start=True,
                         stop=True,
                     )
-                nc.scalar.copy(out=xi_tiles[k][:], in_=bank[:])
+                nc.scalar.copy(out=dst, in_=bank[:])
 
         def quantise(name, src_tile, width, pool, bufs):
             codes = pool.tile([P, width // 4], U32, tag=name + "_codes", name="codes", bufs=bufs, align_bytes=64)
             scales = pool.tile([P, width // 4], U8, tag=name + "_scales", name="scales", bufs=bufs, align_bytes=64)
-            nc.vector.quantize_mx(out=codes[:].bitcast(FP8X4), scales=scales[:], in_=src_tile[:])
+            nc.vector.quantize_mx(out=codes[:].bitcast(FP8X4), scales=scales[:], in_=src_tile)
             return codes, scales
 
         def quant(k):
-            mx[k] = (quantise("gq", gi_tiles[k], 1024, work, 3), quantise("xq", xi_tiles[k], 1024, work, 3))
+            mx[k] = quantise("op", inter[k][:].rearrange("p h c -> p (h c)"), 2048, work, 3)
 
         def mm(bank, left, cols, right, start, stop):
             nc.tensor.matmul_mx(
@@ -165,25 +168,26 @@ def tile_weightedsignedseminmfupdate_t_kernel(tc, x_bytes, x_scale, f, w, g, p, 
             )
 
         def products(k):
-            gq, xq = mx[k]
+            opq = mx[k]
             res = []
-            all_cols = [slice(0, 128), slice(128, 256)]
+            g_cols = [slice(0, 128), slice(128, 256)]
+            x_cols = [slice(256, 384), slice(384, 512)]
             relus = []
             bvs = []
             for j in range(2):
                 bv = psum.tile([P, R], F32, tag="v", name="bv", bufs=2)
-                mm(bv, gq, all_cols[j], b_q, True, True)
+                mm(bv, opq, g_cols[j], b_q, True, True)
                 bvs.append(bv)
                 bu = psum.tile([P, R], F32, tag="u", name="bu", bufs=2)
-                mm(bu, xq, all_cols[j], fw_q, True, True)
+                mm(bu, opq, x_cols[j], fw_q, True, True)
                 a = work.tile([P, R], F32, tag="a", name="a", bufs=4)
                 nc.scalar.activation(out=a[:], in_=bu[:], func=ACT.Relu)
                 relus.append(a)
             for j in range(2):
                 bd = psum.tile([P, R], F32, tag="d", name="bd", bufs=2)
                 bv = bvs[j]
-                mm(bd, xq, all_cols[j], fw_q, True, False)
-                mm(bd, gq, all_cols[j], b_q, False, True)
+                mm(bd, opq, x_cols[j], fw_q, True, False)
+                mm(bd, opq, g_cols[j], b_q, False, True)
                 res.append((relus[j], bv, bd))
             return res
 
@@ -215,6 +219,8 @@ def tile_weightedsignedseminmfupdate_t_kernel(tc, x_bytes, x_scale, f, w, g, p, 
         def times_g(k):
             is_num = batch_of[k] % 2 == 0
             e = num[k] if is_num else den[k]
+            if k < T1_TAIL and TOUCH:
+                nc.vector.tensor_copy(out=touch[:], in_=e[:, 0, 0:1])
             for j in range(2):
                 engine = nc.gpsimd if k < T1_TAIL else nc.vector
                 engine.tensor_tensor(out=e[:, j, :], in0=e[:, j, :], in1=g_tiles[k][:, j, :], op=ALU.mult)
@@ -223,20 +229,28 @@ def tile_weightedsignedseminmfupdate_t_kernel(tc, x_bytes, x_scale, f, w, g, p, 
             is_num = batch_of[k] % 2 == 0
             root((den[k] if is_num else num[k])[:], not is_num)
 
-        def finish(k):
+        def on_gpsimd(k, j):
+            return (2 * k + j) % 4 in G_OUT and k < TAIL
+
+        def finish(k, gpsimd_turn):
             is_num = batch_of[k] % 2 == 0
             e, h = (num[k], den[k]) if is_num else (den[k], num[k])
-            for j in range(2):
-                engine = nc.gpsimd if (2 * k + j) % 4 in G_OUT and k < TAIL else nc.vector
+            halves = [j for j in range(2) if on_gpsimd(k, j) == gpsimd_turn]
+            engine = nc.gpsimd if gpsimd_turn else nc.vector
+            if len(halves) == 2:
+                engine.tensor_tensor(out=e[:], in0=e[:], in1=h[:], op=ALU.mult)
+            elif len(halves) == 1:
+                j = halves[0]
                 engine.tensor_tensor(out=e[:, j, :], in0=e[:, j, :], in1=h[:, j, :], op=ALU.mult)
-                if k >= PAIRS - 2:
-                    nc.sync.dma_start(out=out[256 * k + P * j : 256 * k + P * j + P, :], in_=e[:, j, :])
-            if k < PAIRS - 2:
-                nc.sync.dma_start(out=out[256 * k : 256 * k + 256, :].rearrange("(j p) r -> p j r", p=P), in_=e[:])
+
+        def store(k):
+            e = num[k] if batch_of[k] % 2 == 0 else den[k]
+            nc.sync.dma_start(out=out[256 * k : 256 * k + 256, :].rearrange("(j p) r -> p j r", p=P), in_=e[:])
 
         sgn = keep.tile([P, R], BF16, tag="sgn", name="sgn")
-        nc.vector.tensor_scalar(out=sgn[:], in0=p_row[:, 0, :], scalar1=0.0, scalar2=2.0, op0=ALU.is_ge, op1=ALU.mult)
-        nc.vector.tensor_copy(out=p_row[:, 1, :], in_=p_row[:, 0, :])
+        nc.vector.tensor_scalar(out=sgn[:], in0=p_row[:], scalar1=0.0, scalar2=2.0, op0=ALU.is_ge, op1=ALU.mult)
+        p_cols = keep.tile([P, 1024], BF16, tag="p_cols", name="p_cols")
+        nc.vector.tensor_copy(out=p_cols[:].rearrange("p (n t) -> p n t", t=T), in_=p_col[:].unsqueeze(1).to_broadcast([P, 256, T]))
         nc.vector.tensor_scalar(out=sgn[:], in0=sgn[:], scalar1=-1.0, scalar2=None, op0=ALU.add)
         qn = keep.tile([P, T], F32, tag="qn", name="qn")
         nc.vector.tensor_scalar(out=qn[:], in0=q_col[:], scalar1=-1.0, scalar2=None, op0=ALU.mult)
@@ -249,17 +263,14 @@ def tile_weightedsignedseminmfupdate_t_kernel(tc, x_bytes, x_scale, f, w, g, p, 
         fwt = work.tile([P, T, R], BF16, tag="num", name="fwt", bufs=HOLD, align_bytes=64)
         for t in range(T):
             nc.vector.scalar_tensor_tensor(out=fwt[:, t, :], in0=f_in[:, t, :], scalar=w_col[:, t : t + 1], in1=sgn[:], op0=ALU.mult, op1=ALU.mult)
-        gmul(0, nc.gpsimd)
         fwi = work.tile([P, T * R], BF16, tag="den", name="fwi", bufs=HOLD, align_bytes=64)
         nc.vector.tensor_copy(out=fwi[:].rearrange("p (r t) -> p r t", t=T), in_=fwt[:].rearrange("p t r -> p r t"))
         widen(0, range(T), True)
         weave(0)
         turn(0)
-        emit_turned(0, nc.scalar.copy)
-        gmul(1, nc.gpsimd)
-        fw_q = quantise("fw", fwi, 2048, keep, 1)
-        f_q = quantise("f", fi, 2048, keep, 1)
-        gmul(2, nc.vector)
+        emit_turned(0)
+        fw_q = quantise("fw", fwi[:], 2048, keep, 1)
+        f_q = quantise("f", fi[:], 2048, keep, 1)
         bt = work.tile([P, T, R], BF16, tag="num", name="bt", bufs=HOLD, align_bytes=64)
         banks = []
         for t in range(T):
@@ -272,14 +283,13 @@ def tile_weightedsignedseminmfupdate_t_kernel(tc, x_bytes, x_scale, f, w, g, p, 
         bi = work.tile([P, T * R], BF16, tag="den", name="bi", bufs=HOLD, align_bytes=64)
         nc.vector.tensor_copy(out=bi[:].rearrange("p (r t) -> p r t", t=T), in_=bt[:].rearrange("p t r -> p r t"))
         turn(1)
-        emit_turned(1, nc.scalar.copy)
+        emit_turned(1)
         weave(1)
         quant(0)
-        gmul(3, nc.vector)
-        b_q = quantise("b", bi, 2048, keep, 1)
+        b_q = quantise("b", bi[:], 2048, keep, 1)
         widen(1, range(T), SW1)
         turn(2)
-        emit_turned(2, nc.scalar.copy)
+        emit_turned(2)
         weave(2)
         widen(2, (0, 1), SW2)
 
@@ -309,23 +319,20 @@ def tile_weightedsignedseminmfupdate_t_kernel(tc, x_bytes, x_scale, f, w, g, p, 
                 quant(s + 1)
             if s + 3 < PAIRS:
                 turn(s + 3)
-                if s + 3 not in V_TURN:
-                    emit_turned(s + 3, nc.scalar.copy)
                 weave(s + 3)
-            if s + 4 < PAIRS:
-                gmul(s + 4, nc.vector)
             c = (s + 5) // 2
             if c < N // 512:
-                if s % 2 == 1:
-                    widen(c, (0, 1), False)
-                else:
-                    widen(c, (2, 3), False)
+                for t in (0, 1) if s % 2 == 1 else (2, 3):
+                    widen(c, (t,), t in S_T[c % 2])
             for k in pending:
-                finish(k)
-            pending = new
+                finish(k, False)
             if 2 <= s <= PAIRS + 1:
                 times_g(s - 2)
+            for k in pending:
+                finish(k, True)
+                store(k)
+            pending = new
             if res is not None:
                 parts(s, res)
-            if s + 3 < PAIRS and s + 3 in V_TURN:
-                emit_turned(s + 3, nc.vector.tensor_copy)
+            if s + 3 < PAIRS:
+                emit_turned(s + 3)

from contextlib import ExitStack

import concourse.mybir as mybir
from concourse.masks import make_identity

M, N, R = 512, 8192, 512
FLOPS = 2 * M * N * R + 2 * M * R * R + 2 * N * R * R

F32 = mybir.dt.float32
BF16 = mybir.dt.bfloat16
U32 = mybir.dt.uint32
U8 = mybir.dt.uint8
FP8 = mybir.dt.float8_e4m3fn
FP8X4 = mybir.dt.float8_e4m3fn_x4
ALU = mybir.AluOpType
ACT = mybir.ActivationFunctionType

P = 128
T = 4
PAIRS = N // 256
BATCHES = [5, 9, 9, 7, 2]
DIRECT = 6
LEAD = 7
HOLD = 18
SW1 = True
SW2 = False
S_T = ((1, 2, 3), (2, 3))
TOUCH = True
G_OUT = (3,)
TAIL = 24
T1_TAIL = 30


def tile_weightedsignedseminmfupdate_t_kernel(tc, x_bytes, x_scale, f, w, g, p, q, out):
    nc = tc.nc
    with ExitStack() as ctx:
        keep = ctx.enter_context(tc.tile_pool(name="keep", bufs=1))
        work = ctx.enter_context(tc.tile_pool(name="work", bufs=3))
        psum = ctx.enter_context(tc.psum_pool(name="psum", bufs=2))
        ctx.enter_context(tc.manual_schedule())

        x_tiles = {}
        g_tiles = {}
        wide = {}
        inter = {}
        turned = {}
        mx = {}
        num = {}
        den = {}

        def load_x(h, parts):
            xt = keep.tile([P, T, 1024], U8, tag="x", name="xbytes", bufs=3)
            x_tiles[h] = xt
            wdt = 1024 // parts
            for i in range(parts):
                src_ap = x_bytes[:, h * 1024 + i * wdt : h * 1024 + (i + 1) * wdt].rearrange("(p t) n -> p t n", t=T)
                nc.sync.dma_start(out=xt[:, :, i * wdt : (i + 1) * wdt], in_=src_ap)

        def load_g(k):
            gt = work.tile([P, 2, R], BF16, tag="g", name="gin", bufs=LEAD + 3)
            g_tiles[k] = gt
            nc.sync.dma_start(out=gt[:], in_=g[256 * k : 256 * k + 256, :].rearrange("(j p) r -> p j r", p=P))

        f_in = work.tile([P, T, R], BF16, tag="num", name="f_in", bufs=HOLD, align_bytes=64)
        w_col = keep.tile([P, T], BF16, tag="w_col", name="w_col")
        nc.sync.dma_start(out=w_col[:], in_=w.rearrange("(p t) -> p t", t=T))
        p_row = keep.tile([P, R], BF16, tag="p_row", name="p_row")
        nc.sync.dma_start(out=p_row[:], in_=p.partition_broadcast(P))
        p_col = keep.tile([P, T], BF16, tag="p_col", name="p_col")
        nc.sync.dma_start(out=p_col[:], in_=p.rearrange("(p t) -> p t", t=T))
        nc.sync.dma_start(out=f_in[:], in_=f.rearrange("(p t) r -> p t r", t=T))
        xs = keep.tile([P, T], F32, tag="xs", name="xs")
        nc.sync.dma_start(out=xs[:], in_=x_scale.rearrange("(p t) o -> p (t o)", t=T))
        load_x(0, 2)
        load_g(0)
        q_col = keep.tile([P, T], BF16, tag="q_col", name="q_col")
        nc.sync.dma_start(out=q_col[:], in_=q.rearrange("(p t) -> p t", t=T))
        load_g(1)
        load_g(2)
        load_x(1, 1)
        load_g(3)
        load_x(2, 1)
        for k in range(4, LEAD):
            load_g(k)

        half = keep.tile([P, 1], F32, tag="half", name="half")
        nc.gpsimd.memset(half[:], 0.5)
        ident_f = keep.tile([P, P], F32, tag="ident_f", name="ident_f")
        make_identity(nc, ident_f[:])
        ident_b = keep.tile([P, P], BF16, tag="ident_b", name="ident_b")
        make_identity(nc, ident_b[:])
        touch = keep.tile([P, 1], F32, tag="touch", name="touch")
        warm = keep.tile([P, 1], F32, tag="warm", name="warm")
        nc.scalar.activation(out=warm[:], in_=half[:], func=ACT.Sqrt)

        def widen(c, ts, on_scalar):
            if c not in wide:
                wide[c] = work.tile([P, T, 512], BF16, tag="wide", name="wide", bufs=2)
            xt = x_tiles[c // 2]
            c0 = 512 * (c % 2)
            for t in ts:
                src_ap = xt[:, t, c0 : c0 + 512].bitcast(FP8)
                if on_scalar:
                    nc.scalar.activation(out=wide[c][:, t, :], in_=src_ap, func=ACT.Copy, scale=xs[:, t : t + 1])
                else:
                    nc.vector.tensor_scalar(out=wide[c][:, t, :], in0=src_ap, scalar1=xs[:, t : t + 1], scalar2=None, op0=ALU.mult)

        def inter_tile(k):
            if k not in inter:
                inter[k] = work.tile([P, 2, 1024], BF16, tag="inter", name="inter", bufs=4, align_bytes=64)
            return inter[k]

        def turn(k):
            bank = psum.tile([P, 2, 256], F32, tag="gt", name="gt", bufs=1)
            words = g_tiles[k][:].rearrange("p j r -> p (j r)").bitcast(F32)
            for j in range(2):
                for u in range(2):
                    nc.tensor.transpose(bank[:, u, 128 * j : 128 * j + 128], words[:, 256 * j + u : 256 * (j + 1) : 2], ident_f[:])
            turned[k] = bank

        def emit_turned(k):
            nc.vector.tensor_tensor(
                out=inter_tile(k)[:, 0, :].rearrange("p (n u e) -> p n u e", u=2, e=2),
                in0=turned[k][:].bitcast(BF16).rearrange("p u (n e) -> p n u e", e=2),
                in1=p_cols[:].rearrange("p (n u e) -> p n u e", u=2, e=2),
                op=ALU.mult,
            )

        def weave(k):
            wd = wide[k // 2]
            c0 = 256 * (k % 2)
            dst = inter_tile(k)[:, 1, :]
            if k < DIRECT:
                nc.scalar.copy(
                    out=dst.rearrange("p (n t) -> p n t", t=T),
                    in_=wd[:, :, c0 : c0 + 256].rearrange("p t n -> p n t"),
                )
            else:
                bank = psum.tile([P, 1024], BF16, tag="xw", name="xw", bufs=1)
                for j in range(2):
                    nc.tensor.matmul(
                        bank[:, 512 * j : 512 * j + 512],
                        lhsT=ident_b[:],
                        rhs=wd[:, :, c0 + 128 * j : c0 + 128 * j + 128].rearrange("p t n -> p n t"),
                        start=True,
                        stop=True,
                    )
                nc.scalar.copy(out=dst, in_=bank[:])

        def quantise(name, src_tile, width, pool, bufs):
            codes = pool.tile([P, width // 4], U32, tag=name + "_codes", name="codes", bufs=bufs, align_bytes=64)
            scales = pool.tile([P, width // 4], U8, tag=name + "_scales", name="scales", bufs=bufs, align_bytes=64)
            nc.vector.quantize_mx(out=codes[:].bitcast(FP8X4), scales=scales[:], in_=src_tile)
            return codes, scales

        def quant(k):
            mx[k] = quantise("op", inter[k][:].rearrange("p h c -> p (h c)"), 2048, work, 3)

        def mm(bank, left, cols, right, start, stop):
            nc.tensor.matmul_mx(
                out=bank[:],
                lhsT=left[0][:, cols].bitcast(FP8X4),
                lhsT_scale=left[1][:, cols],
                rhs=right[0][:].bitcast(FP8X4),
                rhs_scale=right[1][:],
                start=start,
                stop=stop,
            )

        def products(k):
            opq = mx[k]
            res = []
            g_cols = [slice(0, 128), slice(128, 256)]
            x_cols = [slice(256, 384), slice(384, 512)]
            relus = []
            bvs = []
            for j in range(2):
                bv = psum.tile([P, R], F32, tag="v", name="bv", bufs=2)
                mm(bv, opq, g_cols[j], b_q, True, True)
                bvs.append(bv)
                bu = psum.tile([P, R], F32, tag="u", name="bu", bufs=2)
                mm(bu, opq, x_cols[j], fw_q, True, True)
                a = work.tile([P, R], F32, tag="a", name="a", bufs=4)
                nc.scalar.activation(out=a[:], in_=bu[:], func=ACT.Relu)
                relus.append(a)
            for j in range(2):
                bd = psum.tile([P, R], F32, tag="d", name="bd", bufs=2)
                bv = bvs[j]
                mm(bd, opq, x_cols[j], fw_q, True, False)
                mm(bd, opq, g_cols[j], b_q, False, True)
                res.append((relus[j], bv, bd))
            return res

        def parts(k, res):
            num[k] = work.tile([P, 2, R], F32, tag="num", name="num", bufs=HOLD, align_bytes=64)
            den[k] = work.tile([P, 2, R], F32, tag="den", name="den", bufs=HOLD, align_bytes=64)
            for j in range(2):
                a, bv, bd = res[j]
                nc.vector.scalar_tensor_tensor(out=num[k][:, j, :], in0=bv[:], scalar=0.0, in1=a[:], op0=ALU.max, op1=ALU.add)
            for j in range(2):
                a, bv, bd = res[j]
                nc.vector.tensor_tensor(out=den[k][:, j, :], in0=num[k][:, j, :], in1=bd[:], op=ALU.subtract)

        batch_of = {}
        k0 = 0
        for b, size in enumerate(BATCHES):
            for i in range(size):
                batch_of[k0 + i] = b
            k0 += size

        def root(tile_ap, is_num):
            nc.scalar.activation(out=tile_ap, in_=tile_ap, func=ACT.Sqrt if is_num else ACT.Abs_reciprocal_sqrt, bias=half[:])

        def first(k):
            is_num = batch_of[k] % 2 == 0
            e = num[k] if is_num else den[k]
            root(e[:], is_num)

        def times_g(k):
            is_num = batch_of[k] % 2 == 0
            e = num[k] if is_num else den[k]
            if k < T1_TAIL and TOUCH:
                nc.vector.tensor_copy(out=touch[:], in_=e[:, 0, 0:1])
            for j in range(2):
                engine = nc.gpsimd if k < T1_TAIL else nc.vector
                engine.tensor_tensor(out=e[:, j, :], in0=e[:, j, :], in1=g_tiles[k][:, j, :], op=ALU.mult)

        def second(k):
            is_num = batch_of[k] % 2 == 0
            root((den[k] if is_num else num[k])[:], not is_num)

        def on_gpsimd(k, j):
            return (2 * k + j) % 4 in G_OUT and k < TAIL

        def finish(k, gpsimd_turn):
            is_num = batch_of[k] % 2 == 0
            e, h = (num[k], den[k]) if is_num else (den[k], num[k])
            halves = [j for j in range(2) if on_gpsimd(k, j) == gpsimd_turn]
            engine = nc.gpsimd if gpsimd_turn else nc.vector
            if len(halves) == 2:
                engine.tensor_tensor(out=e[:], in0=e[:], in1=h[:], op=ALU.mult)
            elif len(halves) == 1:
                j = halves[0]
                engine.tensor_tensor(out=e[:, j, :], in0=e[:, j, :], in1=h[:, j, :], op=ALU.mult)

        def store(k):
            e = num[k] if batch_of[k] % 2 == 0 else den[k]
            nc.sync.dma_start(out=out[256 * k : 256 * k + 256, :].rearrange("(j p) r -> p j r", p=P), in_=e[:])

        sgn = keep.tile([P, R], BF16, tag="sgn", name="sgn")
        nc.vector.tensor_scalar(out=sgn[:], in0=p_row[:], scalar1=0.0, scalar2=2.0, op0=ALU.is_ge, op1=ALU.mult)
        p_cols = keep.tile([P, 1024], BF16, tag="p_cols", name="p_cols")
        nc.vector.tensor_copy(out=p_cols[:].rearrange("p (n t) -> p n t", t=T), in_=p_col[:].unsqueeze(1).to_broadcast([P, 256, T]))
        nc.vector.tensor_scalar(out=sgn[:], in0=sgn[:], scalar1=-1.0, scalar2=None, op0=ALU.add)
        qn = keep.tile([P, T], F32, tag="qn", name="qn")
        nc.vector.tensor_scalar(out=qn[:], in0=q_col[:], scalar1=-1.0, scalar2=None, op0=ALU.mult)

        fi = work.tile([P, T * R], BF16, tag="den", name="fi", bufs=HOLD, align_bytes=64)
        nc.scalar.copy(
            out=fi[:].rearrange("p (t m j) -> p t m j", t=T, j=T),
            in_=f_in[:].rearrange("p j (m t) -> p t m j", t=T),
        )
        fwt = work.tile([P, T, R], BF16, tag="num", name="fwt", bufs=HOLD, align_bytes=64)
        for t in range(T):
            nc.vector.scalar_tensor_tensor(out=fwt[:, t, :], in0=f_in[:, t, :], scalar=w_col[:, t : t + 1], in1=sgn[:], op0=ALU.mult, op1=ALU.mult)
        fwi = work.tile([P, T * R], BF16, tag="den", name="fwi", bufs=HOLD, align_bytes=64)
        nc.vector.tensor_copy(out=fwi[:].rearrange("p (r t) -> p r t", t=T), in_=fwt[:].rearrange("p t r -> p r t"))
        widen(0, range(T), True)
        weave(0)
        turn(0)
        emit_turned(0)
        fw_q = quantise("fw", fwi[:], 2048, keep, 1)
        f_q = quantise("f", fi[:], 2048, keep, 1)
        bt = work.tile([P, T, R], BF16, tag="num", name="bt", bufs=HOLD, align_bytes=64)
        banks = []
        for t in range(T):
            bank = psum.tile([P, R], F32, tag="u" if t % 2 == 0 else "v", name="bb", bufs=2)
            mm(bank, f_q, slice(128 * t, 128 * t + 128), fw_q, True, True)
            if t % 2 == 0:
                nc.scalar.activation(out=bt[:, t, :], in_=bank[:], func=ACT.Copy, scale=qn[:, t : t + 1])
            else:
                nc.vector.tensor_scalar(out=bt[:, t, :], in0=bank[:], scalar1=qn[:, t : t + 1], scalar2=None, op0=ALU.mult)
        bi = work.tile([P, T * R], BF16, tag="den", name="bi", bufs=HOLD, align_bytes=64)
        nc.vector.tensor_copy(out=bi[:].rearrange("p (r t) -> p r t", t=T), in_=bt[:].rearrange("p t r -> p r t"))
        turn(1)
        emit_turned(1)
        weave(1)
        quant(0)
        b_q = quantise("b", bi[:], 2048, keep, 1)
        widen(1, range(T), SW1)
        turn(2)
        emit_turned(2)
        weave(2)
        widen(2, (0, 1), SW2)

        starts = [sum(BATCHES[:b]) for b in range(len(BATCHES) + 1)]
        todo = {}
        for b in range(len(BATCHES)):
            size = BATCHES[b]
            room = BATCHES[b + 1] if b + 1 < len(BATCHES) else size
            for i in range(size):
                step = starts[b + 1] + 1 + (i * room) // size
                todo.setdefault(step, []).append(starts[b] + i)
        last = max(todo)
        pending = []
        load_x(3, 1)
        for s in range(last + 2):
            if s + LEAD < PAIRS:
                load_g(s + LEAD)
            if s % 4 == 3 and s // 4 + 4 < 8:
                load_x(s // 4 + 4, 1)
            res = products(s) if s < PAIRS else None
            new = todo.get(s, [])
            for k in new:
                second(k)
            if 1 <= s <= PAIRS:
                first(s - 1)
            if s + 1 < PAIRS:
                quant(s + 1)
            if s + 3 < PAIRS:
                turn(s + 3)
                weave(s + 3)
            c = (s + 5) // 2
            if c < N // 512:
                for t in (0, 1) if s % 2 == 1 else (2, 3):
                    widen(c, (t,), t in S_T[c % 2])
            for k in pending:
                finish(k, False)
            if 2 <= s <= PAIRS + 1:
                times_g(s - 2)
            for k in pending:
                finish(k, True)
                store(k)
            pending = new
            if res is not None:
                parts(s, res)
            if s + 3 < PAIRS:
                emit_turned(s + 3)
